import numpy as np
import ml_dtypes

BF16 = ml_dtypes.bfloat16


def bf(x):
    return np.asarray(x, np.float32).astype(BF16)


def f32(x):
    return np.asarray(x, np.float32)


def f64(x):
    return np.asarray(x).astype(np.float64)


def striped(idx):
    return np.tile(idx.reshape(-1, 16).T, (8, 1))


S, K, M, N, D, V = 1024, 256, 256, 2048, 8, 256


def setup_inputs():
    return {"table": bf(np.random.standard_normal((K, S))), "w": bf(np.random.standard_normal((K, M)) / np.sqrt(K)), "b": f32(0.5 * np.random.standard_normal((M, 1))), "offs": striped(np.random.permutation(np.tile(np.arange(S), 2))[:N])}


def reference(table, w, b, offs):
    idx = offs[:16].T.reshape(-1)
    x = f64(table)[:, idx]
    y = f64(w).T @ x
    z = np.maximum(y + f64(b), 0.0)
    return z.reshape(M, V, D).max(axis=2)

@@ -1,0 +1,71 @@
+import concourse.mybir as mybir
+
+BF16, F32, U16 = mybir.dt.bfloat16, mybir.dt.float32, mybir.dt.uint16
+
+P = 128
+S = 1024
+K = 256
+M = 256
+N = 2048
+GROUP = 8
+V = N // GROUP
+K_BLOCKS = K // P
+M_BLOCKS = M // P
+PIECE = 512
+PIECES = N // PIECE
+PIECE_OFFSET_COLUMNS = PIECE // 16
+PIECE_NODES = PIECE // GROUP
+
+FLOPS = 2 * K * M * N
+
+
+def tile_gather_matmul_kernel(tc, table, w, b, offs, out):
+    nc = tc.nc
+    with (
+        tc.tile_pool(name="held", bufs=1) as held,
+        tc.tile_pool(name="small", bufs=M_BLOCKS * PIECES) as small,
+        tc.psum_pool(name="banks", bufs=M_BLOCKS * PIECES) as banks,
+    ):
+        offsets = held.tile([P, N // 16], U16, name="offsets")
+        weight_blocks = [held.tile([P, M], BF16, name=f"weight_block{kb}") for kb in range(K_BLOCKS)]
+        table_blocks = [held.tile([P, S], BF16, name=f"table_block{kb}") for kb in range(K_BLOCKS)]
+        bias = held.tile([P, M_BLOCKS], F32, name="bias")
+        nc.sync.dma_start(offsets[:], offs)
+        nc.sync.dma_start(weight_blocks[0][:], w[0:P, :])
+        nc.scalar.dma_start(table_blocks[0][:], table[0:P, :])
+        for kb in range(1, K_BLOCKS):
+            nc.scalar.dma_start(weight_blocks[kb][:], w[kb * P : (kb + 1) * P, :])
+            nc.scalar.dma_start(table_blocks[kb][:], table[kb * P : (kb + 1) * P, :])
+        nc.scalar.dma_start(bias[:], b.rearrange("(mb p) o -> p (mb o)", p=P))
+
+        for mb in range(M_BLOCKS):
+            for piece in range(PIECES):
+                piece_offsets = offsets[:, piece * PIECE_OFFSET_COLUMNS : (piece + 1) * PIECE_OFFSET_COLUMNS]
+                bank = banks.tile([P, PIECE], F32, name="bank")
+                for kb in range(K_BLOCKS):
+                    nc.tensor.matmul(
+                        bank[:],
+                        weight_blocks[kb][:, mb * P : (mb + 1) * P],
+                        table_blocks[kb][:].indirect(piece_offsets),
+                        start=(kb == 0),
+                        stop=(kb == K_BLOCKS - 1),
+                    )
+                largest = small.tile([P, PIECE_NODES], F32, name="largest")
+                nc.vector.tensor_reduce(
+                    out=largest[:],
+                    in_=bank[:].rearrange("p (v g) -> p v g", g=GROUP),
+                    axis=mybir.AxisListType.X,
+                    op=mybir.AluOpType.max,
+                )
+                pooled = small.tile([P, PIECE_NODES], F32, name="pooled")
+                nc.vector.tensor_scalar(
+                    out=pooled[:],
+                    in0=largest[:],
+                    scalar1=bias[:, mb : mb + 1],
+                    scalar2=0.0,
+                    op0=mybir.AluOpType.add,
+                    op1=mybir.AluOpType.max,
+                )
+                nc.sync.dma_start(
+                    out[mb * P : (mb + 1) * P, piece * PIECE_NODES : (piece + 1) * PIECE_NODES], pooled[:]
+                )

@@ -3,6 +3,7 @@ import concourse.mybir as mybir
 BF16, F32, U16 = mybir.dt.bfloat16, mybir.dt.float32, mybir.dt.uint16
 
 P = 128
+DMA_ALIGN = 256
 S = 1024
 K = 256
 M = 256
@@ -26,9 +27,13 @@ def tile_gather_matmul_kernel(tc, table, w, b, offs, out):
         tc.tile_pool(name="small", bufs=M_BLOCKS * PIECES) as small,
         tc.psum_pool(name="banks", bufs=M_BLOCKS * PIECES) as banks,
     ):
-        offsets = held.tile([P, N // 16], U16, name="offsets")
-        weight_blocks = [held.tile([P, M], BF16, name=f"weight_block{kb}") for kb in range(K_BLOCKS)]
-        table_blocks = [held.tile([P, S], BF16, name=f"table_block{kb}") for kb in range(K_BLOCKS)]
+        offsets = held.tile([P, N // 16], U16, name="offsets", align_bytes=DMA_ALIGN)
+        weight_blocks = [
+            held.tile([P, M], BF16, name=f"weight_block{kb}", align_bytes=DMA_ALIGN) for kb in range(K_BLOCKS)
+        ]
+        table_blocks = [
+            held.tile([P, S], BF16, name=f"table_block{kb}", align_bytes=DMA_ALIGN) for kb in range(K_BLOCKS)
+        ]
         bias = held.tile([P, M_BLOCKS], F32, name="bias")
         nc.sync.dma_start(offsets[:], offs)
         nc.sync.dma_start(weight_blocks[0][:], w[0:P, :])
@@ -57,7 +62,7 @@ def tile_gather_matmul_kernel(tc, table, w, b, offs, out):
                     axis=mybir.AxisListType.X,
                     op=mybir.AluOpType.max,
                 )
-                pooled = small.tile([P, PIECE_NODES], F32, name="pooled")
+                pooled = small.tile([P, PIECE_NODES], F32, name="pooled", align_bytes=DMA_ALIGN)
                 nc.vector.tensor_scalar(
                     out=pooled[:],
                     in0=largest[:],

@@ -29,18 +29,22 @@ def tile_gather_matmul_kernel(tc, table, w, b, offs, out):
     ):
         offsets = held.tile([P, N // 16], U16, name="offsets", align_bytes=DMA_ALIGN)
         weight_blocks = [
-            held.tile([P, M], BF16, name=f"weight_block{kb}", align_bytes=DMA_ALIGN) for kb in range(K_BLOCKS)
+            [held.tile([P, P], BF16, name=f"weight_block{kb}_{mb}", align_bytes=DMA_ALIGN) for mb in range(M_BLOCKS)]
+            for kb in range(K_BLOCKS)
         ]
         table_blocks = [
             held.tile([P, S], BF16, name=f"table_block{kb}", align_bytes=DMA_ALIGN) for kb in range(K_BLOCKS)
         ]
         bias = held.tile([P, M_BLOCKS], F32, name="bias")
         nc.sync.dma_start(offsets[:], offs)
-        nc.sync.dma_start(weight_blocks[0][:], w[0:P, :])
+        nc.sync.dma_start(weight_blocks[0][0][:], w[0:P, 0:P])
         nc.scalar.dma_start(table_blocks[0][:], table[0:P, :])
         for kb in range(1, K_BLOCKS):
-            nc.scalar.dma_start(weight_blocks[kb][:], w[kb * P : (kb + 1) * P, :])
+            nc.scalar.dma_start(weight_blocks[kb][0][:], w[kb * P : (kb + 1) * P, 0:P])
             nc.scalar.dma_start(table_blocks[kb][:], table[kb * P : (kb + 1) * P, :])
+        for mb in range(1, M_BLOCKS):
+            for kb in range(K_BLOCKS):
+                nc.scalar.dma_start(weight_blocks[kb][mb][:], w[kb * P : (kb + 1) * P, mb * P : (mb + 1) * P])
         nc.scalar.dma_start(bias[:], b.rearrange("(mb p) o -> p (mb o)", p=P))
 
         for mb in range(M_BLOCKS):
@@ -50,7 +54,7 @@ def tile_gather_matmul_kernel(tc, table, w, b, offs, out):
                 for kb in range(K_BLOCKS):
                     nc.tensor.matmul(
                         bank[:],
-                        weight_blocks[kb][:, mb * P : (mb + 1) * P],
+                        weight_blocks[kb][mb][:],
                         table_blocks[kb][:].indirect(piece_offsets),
                         start=(kb == 0),
                         stop=(kb == K_BLOCKS - 1),

@@ -36,16 +36,16 @@ def tile_gather_matmul_kernel(tc, table, w, b, offs, out):
             held.tile([P, S], BF16, name=f"table_block{kb}", align_bytes=DMA_ALIGN) for kb in range(K_BLOCKS)
         ]
         bias = held.tile([P, M_BLOCKS], F32, name="bias")
+        nc.sync.dma_start(table_blocks[0][:], table[0:P, :])
         nc.sync.dma_start(offsets[:], offs)
         nc.sync.dma_start(weight_blocks[0][0][:], w[0:P, 0:P])
-        nc.scalar.dma_start(table_blocks[0][:], table[0:P, :])
         for kb in range(1, K_BLOCKS):
-            nc.scalar.dma_start(weight_blocks[kb][0][:], w[kb * P : (kb + 1) * P, 0:P])
-            nc.scalar.dma_start(table_blocks[kb][:], table[kb * P : (kb + 1) * P, :])
+            nc.sync.dma_start(weight_blocks[kb][0][:], w[kb * P : (kb + 1) * P, 0:P])
+            nc.sync.dma_start(table_blocks[kb][:], table[kb * P : (kb + 1) * P, :])
         for mb in range(1, M_BLOCKS):
             for kb in range(K_BLOCKS):
-                nc.scalar.dma_start(weight_blocks[kb][mb][:], w[kb * P : (kb + 1) * P, mb * P : (mb + 1) * P])
-        nc.scalar.dma_start(bias[:], b.rearrange("(mb p) o -> p (mb o)", p=P))
+                nc.sync.dma_start(weight_blocks[kb][mb][:], w[kb * P : (kb + 1) * P, mb * P : (mb + 1) * P])
+        nc.sync.dma_start(bias[:], b.rearrange("(mb p) o -> p (mb o)", p=P))
 
         for mb in range(M_BLOCKS):
             for piece in range(PIECES):

import concourse.mybir as mybir

BF16, F32, U16 = mybir.dt.bfloat16, mybir.dt.float32, mybir.dt.uint16

P = 128
DMA_ALIGN = 256
S = 1024
K = 256
M = 256
N = 2048
GROUP = 8
V = N // GROUP
K_BLOCKS = K // P
M_BLOCKS = M // P
PIECE = 512
PIECES = N // PIECE
PIECE_OFFSET_COLUMNS = PIECE // 16
PIECE_NODES = PIECE // GROUP

FLOPS = 2 * K * M * N


def tile_gather_matmul_kernel(tc, table, w, b, offs, out):
    nc = tc.nc
    with (
        tc.tile_pool(name="held", bufs=1) as held,
        tc.tile_pool(name="small", bufs=M_BLOCKS * PIECES) as small,
        tc.psum_pool(name="banks", bufs=M_BLOCKS * PIECES) as banks,
    ):
        offsets = held.tile([P, N // 16], U16, name="offsets", align_bytes=DMA_ALIGN)
        weight_blocks = [
            [held.tile([P, P], BF16, name=f"weight_block{kb}_{mb}", align_bytes=DMA_ALIGN) for mb in range(M_BLOCKS)]
            for kb in range(K_BLOCKS)
        ]
        table_blocks = [
            held.tile([P, S], BF16, name=f"table_block{kb}", align_bytes=DMA_ALIGN) for kb in range(K_BLOCKS)
        ]
        bias = held.tile([P, M_BLOCKS], F32, name="bias")
        nc.sync.dma_start(table_blocks[0][:], table[0:P, :])
        nc.sync.dma_start(offsets[:], offs)
        nc.sync.dma_start(weight_blocks[0][0][:], w[0:P, 0:P])
        for kb in range(1, K_BLOCKS):
            nc.sync.dma_start(weight_blocks[kb][0][:], w[kb * P : (kb + 1) * P, 0:P])
            nc.sync.dma_start(table_blocks[kb][:], table[kb * P : (kb + 1) * P, :])
        for mb in range(1, M_BLOCKS):
            for kb in range(K_BLOCKS):
                nc.sync.dma_start(weight_blocks[kb][mb][:], w[kb * P : (kb + 1) * P, mb * P : (mb + 1) * P])
        nc.sync.dma_start(bias[:], b.rearrange("(mb p) o -> p (mb o)", p=P))

        for mb in range(M_BLOCKS):
            for piece in range(PIECES):
                piece_offsets = offsets[:, piece * PIECE_OFFSET_COLUMNS : (piece + 1) * PIECE_OFFSET_COLUMNS]
                bank = banks.tile([P, PIECE], F32, name="bank")
                for kb in range(K_BLOCKS):
                    nc.tensor.matmul(
                        bank[:],
                        weight_blocks[kb][mb][:],
                        table_blocks[kb][:].indirect(piece_offsets),
                        start=(kb == 0),
                        stop=(kb == K_BLOCKS - 1),
                    )
                largest = small.tile([P, PIECE_NODES], F32, name="largest")
                nc.vector.tensor_reduce(
                    out=largest[:],
                    in_=bank[:].rearrange("p (v g) -> p v g", g=GROUP),
                    axis=mybir.AxisListType.X,
                    op=mybir.AluOpType.max,
                )
                pooled = small.tile([P, PIECE_NODES], F32, name="pooled", align_bytes=DMA_ALIGN)
                nc.vector.tensor_scalar(
                    out=pooled[:],
                    in0=largest[:],
                    scalar1=bias[:, mb : mb + 1],
                    scalar2=0.0,
                    op0=mybir.AluOpType.add,
                    op1=mybir.AluOpType.max,
                )
                nc.sync.dma_start(
                    out[mb * P : (mb + 1) * P, piece * PIECE_NODES : (piece + 1) * PIECE_NODES], pooled[:]
                )
